import numpy as np
import ml_dtypes


def mxq(x, axis, fmt="e4m3"):
    dtype, down = {"e4m3": (ml_dtypes.float8_e4m3fn, 7), "e5m2": (ml_dtypes.float8_e5m2, 14)}[fmt]
    v = np.moveaxis(np.asarray(x, np.float32).astype(ml_dtypes.bfloat16).astype(np.float64), axis, -1)
    blocks = v.reshape(v.shape[:-1] + (-1, 32))
    amax = np.abs(blocks).max(-1, keepdims=True)
    byte = np.maximum(np.where(amax > 0, np.frexp(amax)[1] - 1 + 127, 0) - down, 1)
    scale = np.exp2(byte - 127.0)
    codes = (blocks / scale).astype(np.float32).astype(dtype).astype(np.float64)
    return np.moveaxis((codes * scale).reshape(v.shape), -1, axis)


WIDE = False


def mx_kscale(k):
    if not WIDE:
        return np.ones(k)
    levels = np.array([10, -10, 5, -5, 0])
    if k % 512:
        return np.exp2(np.random.permutation(np.resize(levels, k // 32))).repeat(32)
    a = np.empty((k // 512, 16))
    for p in range(k // 512):
        a[p, :8] = np.random.permutation(np.resize(levels, 8))
        for g in range(8):
            far = levels[np.abs(levels - a[p, g]) >= 10]
            a[p, g + 8] = far[np.random.randint(len(far))]
    return np.exp2(a.ravel()).repeat(32)


def f64(x):
    return np.asarray(x).astype(np.float64)


def striped(idx):
    return np.tile(idx.reshape(-1, 16).T, (8, 1)).astype(np.uint16)


def unstriped(offs):
    return offs[:16].T.reshape(-1).astype(np.int64)


def pack_weight(w):
    k, n = w.shape
    w = f64(np.asarray(w, np.float32).astype(ml_dtypes.bfloat16)).reshape(k // 32, 32, n)
    amax = np.abs(w).max(1)
    byte = np.clip(np.where(amax > 0, np.frexp(amax)[1] - 1 + 127 - 7, 1), 1, 254)
    scaled = (w * np.exp2(127.0 - byte)[:, None, :]).reshape(k, n).astype(np.float32)
    words = np.ascontiguousarray(scaled.reshape(k // 512, 128, 4, n).transpose(0, 1, 3, 2)).astype(ml_dtypes.float8_e4m3fn).view(np.uint8)
    return words, np.ascontiguousarray(byte.astype(np.uint8).reshape(k // 512, 16, n))


def unpack_weight(words, scales):
    g, p, n, _ = words.shape
    vals = np.ascontiguousarray(words).view(ml_dtypes.float8_e4m3fn).astype(np.float64) * np.repeat(np.exp2(scales.astype(np.float64) - 127.0), 8, axis=1)[..., None]
    return vals.transpose(0, 1, 3, 2).reshape(g * 512, n)


K, T, D, S, V, N = 512, 2048, 4, 1024, 512, 256


def setup_inputs():
    n = np.random.standard_normal
    s = mx_kscale(K)[:, None]
    packed = pack_weight(n((K, T)) * s)
    return {
        "x_words": packed[0],
        "x_scales": packed[1],
        "w": (n((K, N)) / np.sqrt(K) / s).astype(np.float32),
        "gate": np.tile(np.random.uniform(0.2, 1.0, (D, 1, V)) / np.sqrt(D), (1, N, 1)).astype(np.float32),
        "offs": striped(np.random.permutation(T)[:S]),
        "pos1": striped(np.random.permutation(S)[:V]),
        "pos2": striped(np.random.permutation(S)[:V]),
        "pos3": striped(np.random.permutation(S)[:V]),
        "pos4": striped(np.random.permutation(S)[:V]),
    }


def reference(x_words, x_scales, w, gate, offs, pos1, pos2, pos3, pos4):
    idx = unstriped(offs)
    xq = unpack_weight(x_words, x_scales)[:, idx]
    y = mxq(f64(w), 0, "e4m3").T @ xq
    return sum(f64(gate[d]) * y[:, unstriped(p)] for d, p in enumerate((pos1, pos2, pos3, pos4)))

@@ -1,0 +1,172 @@
+from contextlib import ExitStack
+
+import concourse.mybir as mybir
+from concourse.masks import make_identity
+
+K, T, D, S, V, N = 512, 2048, 4, 1024, 512, 256
+FLOPS = 2 * K * N * S
+BYTES = 128 * T * 4 + 16 * T + K * N * 4 + D * V * 4 + N * V * 4 + 128 * (S + D * V) // 16 * 2
+
+F32 = mybir.dt.float32
+BF16 = mybir.dt.bfloat16
+I32 = mybir.dt.int32
+U32 = mybir.dt.uint32
+U16 = mybir.dt.uint16
+U8 = mybir.dt.uint8
+FP8X4 = mybir.dt.float8_e4m3fn_x4
+MULT = mybir.AluOpType.mult
+ADD = mybir.AluOpType.add
+
+P = 128
+PACK = 4
+LANES = 16
+Q = 256
+H = V // 2
+
+
+def tile_picked_sub_lin_none_sub_p_kernel(
+    tc, x_words, x_scales, w, gate, offs, pos1, pos2, pos3, pos4, out
+):
+    nc = tc.nc
+    with ExitStack() as ctx:
+        lists = ctx.enter_context(tc.tile_pool(name="lists", bufs=1))
+        keep = ctx.enter_context(tc.tile_pool(name="keep", bufs=1))
+        psum = ctx.enter_context(tc.psum_pool(name="psum", bufs=1))
+
+        offs_t = lists.tile([P, S // LANES], U16, name="offs_t")
+        pos_t = [lists.tile([P, V // LANES], U16, name="pos_t%d" % d) for d in range(D)]
+        pos_in = (pos1, pos2, pos3, pos4)
+
+        scale_win = keep.tile([P, T], U8, name="scale_win", align_bytes=64)
+        ident = keep.tile([P, P], F32, name="ident")
+        nc.vector.memset(scale_win[:].bitcast(I32), 0)
+        nc.vector.memset(ident[:], 0.0)
+        make_identity(nc, ident[:], nomemset=True)
+
+        nc.sync.dma_start(offs_t[:], offs)
+        nc.sync.dma_start(pos_t[0][:], pos_in[0])
+        nc.sync.dma_start(pos_t[1][:], pos_in[1])
+        for q in range(4):
+            eng = nc.sync if q < 2 else nc.scalar
+            eng.dma_start(scale_win[32 * q : 32 * q + 4, :].bitcast(I32), x_scales[0, 4 * q : 4 * q + 4, :].bitcast(I32))
+        word_win = keep.tile([P, T], I32, name="word_win")
+        nc.sync.dma_start(word_win[:], x_words[0].rearrange("p c r -> p (c r)").bitcast(I32))
+        w_rows = w.rearrange("(p j) m -> p j m", j=PACK)
+        w_raw = [keep.tile([P, PACK, P], F32, name="w_raw%d" % b) for b in range(2)]
+        for b in range(2):
+            nc.sync.dma_start(w_raw[b][:], w_rows[:, :, b * P : (b + 1) * P])
+        gate_t = [keep.tile([P, V], F32, name="gate_t%d" % d) for d in range(D)]
+        for d in range(D):
+            if d >= 2:
+                nc.sync.dma_start(pos_t[d][:], pos_in[d])
+            nc.sync.dma_start(gate_t[d][:], gate[d, 0:P, :])
+
+        x_scale = keep.tile([P, S], U8, name="x_scale", align_bytes=64)
+        nc.vector.tensor_copy(x_scale[:], scale_win[:].indirect(offs_t[:]))
+
+        def gather_words(tile, start, count):
+            nc.vector.tensor_copy(
+                tile[:], word_win[:].bitcast(U32).indirect(offs_t[:, start // LANES : (start + count) // LANES])
+            )
+
+        w_code = [keep.tile([P, P], U32, name="w_code%d" % b, align_bytes=64) for b in range(2)]
+        w_scale = [keep.tile([P, P], U8, name="w_scale%d" % b, align_bytes=64) for b in range(2)]
+
+        def quantize(b, tag):
+            grouped = keep.tile([P, P, PACK], BF16, name="grouped%d" % b, tag=tag, align_bytes=64)
+            nc.scalar.copy(grouped[:], w_raw[b][:].rearrange("p j m -> p m j"))
+            nc.vector.quantize_mx(
+                out=w_code[b][:].bitcast(FP8X4), scales=w_scale[b][:], in_=grouped[:].rearrange("p m j -> p (m j)")
+            )
+
+        x_a = keep.tile([P, 2 * Q], U32, name="x_a", align_bytes=64)
+        x_b = keep.tile([P, Q], U32, name="x_b", align_bytes=64)
+        gather_words(x_a, 0, 2 * Q)
+        gather_words(x_b, 2 * Q, Q)
+        quantize(0, "held")
+        x_c = keep.tile([P, Q], U32, name="x_c", tag="held", align_bytes=64)
+        gather_words(x_c, 3 * Q, Q)
+        quantize(1, "grouped1")
+        x_code = [x_a[:, 0:Q], x_a[:, Q : 2 * Q], x_b[:], x_c[:]]
+
+        y = [keep.tile([P, S], F32, name="y%d" % b) for b in range(2)]
+
+        def product(b, acc, codes, start, count):
+            nc.tensor.matmul_mx(
+                out=acc,
+                lhsT=w_code[b][:].bitcast(FP8X4),
+                lhsT_scale=w_scale[b][:],
+                rhs=codes.bitcast(FP8X4),
+                rhs_scale=x_scale[:, start : start + count],
+                start=True,
+                stop=True,
+            )
+
+        for i in range(4):
+            acc = psum.tile([P, Q], F32, name="acc0_%d" % i, tag="bank%d" % i)
+            product(0, acc[:], x_code[i], i * Q, Q)
+            if i % 2 == 0:
+                nc.scalar.copy(y[0][:, i * Q : (i + 1) * Q], acc[:])
+            else:
+                nc.vector.tensor_copy(y[0][:, i * Q : (i + 1) * Q], acc[:])
+        acc = psum.tile([P, 2 * Q], F32, name="acc1_0", tag="bank4")
+        product(1, acc[:], x_a[:], 0, 2 * Q)
+        nc.scalar.copy(y[1][:, 0 : 2 * Q], acc[:])
+        acc = psum.tile([P, 2 * Q], F32, name="acc1_1", tag="bank5")
+        product(1, acc[:, 0:Q], x_code[2], 2 * Q, Q)
+        product(1, acc[:, Q : 2 * Q], x_code[3], 3 * Q, Q)
+        nc.scalar.copy(y[1][:, 2 * Q : 4 * Q], acc[:])
+
+        def gated(b, d, v0, count):
+            term = keep.tile([P, count], F32, name="term%d_%d_%d" % (b, d, v0))
+            nc.vector.tensor_tensor(
+                term[:],
+                y[b][:].indirect(pos_t[d][:, v0 // LANES : (v0 + count) // LANES]),
+                gate_t[d][:, v0 : v0 + count],
+                MULT,
+            )
+            return term
+
+        def add_turned(bank, term, first, last):
+            chunks = term.shape[1] // P
+            for c in range(chunks):
+                nc.tensor.matmul(
+                    bank[:, c * P : (c + 1) * P],
+                    term[:, c * P : (c + 1) * P],
+                    ident[:],
+                    start=first and c == 0,
+                    stop=last and c == chunks - 1,
+                    is_transpose=True,
+                )
+
+        def turn_back(bank, name, tag):
+            width = bank.shape[1]
+            staged = keep.tile([P, width], F32, name="staged" + name)
+            nc.scalar.copy(staged[:], bank[:])
+            back = psum.tile([P, width], F32, name="back" + name, tag=tag)
+            for c in range(width // P):
+                nc.tensor.transpose(back[:, c * P : (c + 1) * P], staged[:, c * P : (c + 1) * P], ident[:])
+            return back
+
+        sum0 = psum.tile([P, V], F32, name="sum0", tag="bank6")
+        for d in range(D):
+            add_turned(sum0[:], gated(0, d, 0, V)[:], d == 0, d == D - 1)
+        back0 = turn_back(sum0[:], "0", "bank1")
+        res0 = keep.tile([P, V], F32, name="res0")
+        nc.scalar.copy(res0[:], back0[:])
+        nc.sync.dma_start(out[0:P, :], res0[:])
+
+        sum1 = [psum.tile([P, H], F32, name="sum1_%d" % h, tag=("bank7", "bank0")[h]) for h in range(2)]
+        for d in range(D - 2):
+            term = gated(1, d, 0, V)
+            for h in range(2):
+                add_turned(sum1[h][:], term[:, h * H : (h + 1) * H], d == 0, False)
+        back1 = []
+        for h in range(2):
+            add_turned(sum1[h][:], gated(1, D - 2, h * H, H)[:], False, True)
+            back1.append(turn_back(sum1[h][:], "1_%d" % h, "bank%d" % (2 + h)))
+        last = [gated(1, D - 1, h * H, H) for h in range(2)]
+        for h in range(2):
+            res1 = keep.tile([P, H], F32, name="res1_%d" % h)
+            nc.vector.tensor_tensor(res1[:], last[h][:], back1[h][:], ADD)
+            nc.sync.dma_start(out[P : 2 * P, h * H : (h + 1) * H], res1[:])

@@ -49,72 +49,77 @@ def tile_picked_sub_lin_none_sub_p_kernel(
         for q in range(4):
             eng = nc.sync if q < 2 else nc.scalar
             eng.dma_start(scale_win[32 * q : 32 * q + 4, :].bitcast(I32), x_scales[0, 4 * q : 4 * q + 4, :].bitcast(I32))
-        word_win = keep.tile([P, T], I32, name="word_win")
+        word_win = keep.tile([P, T], I32, name="word_win", tag="word_slot", align_bytes=64)
         nc.sync.dma_start(word_win[:], x_words[0].rearrange("p c r -> p (c r)").bitcast(I32))
         w_rows = w.rearrange("(p j) m -> p j m", j=PACK)
         w_raw = [keep.tile([P, PACK, P], F32, name="w_raw%d" % b) for b in range(2)]
         for b in range(2):
             nc.sync.dma_start(w_raw[b][:], w_rows[:, :, b * P : (b + 1) * P])
-        gate_t = [keep.tile([P, V], F32, name="gate_t%d" % d) for d in range(D)]
-        for d in range(D):
-            if d >= 2:
-                nc.sync.dma_start(pos_t[d][:], pos_in[d])
-            nc.sync.dma_start(gate_t[d][:], gate[d, 0:P, :])
+        nc.sync.dma_start(pos_t[2][:], pos_in[2])
+        nc.sync.dma_start(pos_t[3][:], pos_in[3])
+        gate_t = keep.tile([P, D, V], F32, name="gate_t")
+        nc.sync.dma_start(gate_t[:], gate[:, 0:P, :].rearrange("d p v -> p d v"))
 
         x_scale = keep.tile([P, S], U8, name="x_scale", align_bytes=64)
         nc.vector.tensor_copy(x_scale[:], scale_win[:].indirect(offs_t[:]))
 
-        def gather_words(tile, start, count):
+        def gather_words(start, count, tag):
+            tile = keep.tile([P, count], U32, name="x_code%d" % start, tag=tag, align_bytes=64)
             nc.vector.tensor_copy(
                 tile[:], word_win[:].bitcast(U32).indirect(offs_t[:, start // LANES : (start + count) // LANES])
             )
+            return tile
 
-        w_code = [keep.tile([P, P], U32, name="w_code%d" % b, align_bytes=64) for b in range(2)]
-        w_scale = [keep.tile([P, P], U8, name="w_scale%d" % b, align_bytes=64) for b in range(2)]
-
-        def quantize(b, tag):
-            grouped = keep.tile([P, P, PACK], BF16, name="grouped%d" % b, tag=tag, align_bytes=64)
-            nc.scalar.copy(grouped[:], w_raw[b][:].rearrange("p j m -> p m j"))
-            nc.vector.quantize_mx(
-                out=w_code[b][:].bitcast(FP8X4), scales=w_scale[b][:], in_=grouped[:].rearrange("p m j -> p (m j)")
+        def quantize(b, in_tag, out_tag):
+            grouped = keep.tile([P, P, PACK], BF16, name="grouped%d" % b, tag=in_tag, align_bytes=64)
+            nc.scalar.copy(
+                grouped[:].rearrange("p (c i) j -> p c j i", i=PACK),
+                w_raw[b][:].rearrange("p j (c i) -> p c j i", i=PACK),
             )
+            code = keep.tile([P, P], U32, name="w_code%d" % b, tag=out_tag, align_bytes=64)
+            scale = keep.tile([P, P], U8, name="w_scale%d" % b, align_bytes=64)
+            nc.vector.quantize_mx(
+                out=code[:].bitcast(FP8X4), scales=scale[:], in_=grouped[:].rearrange("p m j -> p (m j)")
+            )
+            return code, scale
 
-        x_a = keep.tile([P, 2 * Q], U32, name="x_a", align_bytes=64)
-        x_b = keep.tile([P, Q], U32, name="x_b", align_bytes=64)
-        gather_words(x_a, 0, 2 * Q)
-        gather_words(x_b, 2 * Q, Q)
-        quantize(0, "held")
-        x_c = keep.tile([P, Q], U32, name="x_c", tag="held", align_bytes=64)
-        gather_words(x_c, 3 * Q, Q)
-        quantize(1, "grouped1")
-        x_code = [x_a[:, 0:Q], x_a[:, Q : 2 * Q], x_b[:], x_c[:]]
+        x_a = gather_words(0, 2 * Q, "x_a")
+        x_b = gather_words(2 * Q, Q, "x_b")
+        w_mx = [quantize(0, "held", "w_code0")]
+        x_c = gather_words(3 * Q, Q, "held")
+        w_mx.append(quantize(1, "grouped1", "word_slot"))
 
         y = [keep.tile([P, S], F32, name="y%d" % b) for b in range(2)]
 
-        def product(b, acc, codes, start, count):
+        def product(b, acc, codes, start):
+            code, scale = w_mx[b]
             nc.tensor.matmul_mx(
                 out=acc,
-                lhsT=w_code[b][:].bitcast(FP8X4),
-                lhsT_scale=w_scale[b][:],
+                lhsT=code[:].bitcast(FP8X4),
+                lhsT_scale=scale[:],
                 rhs=codes.bitcast(FP8X4),
-                rhs_scale=x_scale[:, start : start + count],
+                rhs_scale=x_scale[:, start : start + codes.shape[1]],
                 start=True,
                 stop=True,
             )
 
-        for i in range(4):
-            acc = psum.tile([P, Q], F32, name="acc0_%d" % i, tag="bank%d" % i)
-            product(0, acc[:], x_code[i], i * Q, Q)
-            if i % 2 == 0:
-                nc.scalar.copy(y[0][:, i * Q : (i + 1) * Q], acc[:])
+        pieces = [x_a[:, 0:Q], x_a[:, Q : 2 * Q], x_b[:], x_c[:, 0:P], x_c[:, P:Q]]
+        start = 0
+        for i, codes in enumerate(pieces):
+            count = codes.shape[1]
+            acc = psum.tile([P, count], F32, name="acc0_%d" % i, tag="bank%d" % i)
+            product(0, acc[:], codes, start)
+            if i in (0, 2, 3):
+                nc.scalar.copy(y[0][:, start : start + count], acc[:])
             else:
-                nc.vector.tensor_copy(y[0][:, i * Q : (i + 1) * Q], acc[:])
-        acc = psum.tile([P, 2 * Q], F32, name="acc1_0", tag="bank4")
-        product(1, acc[:], x_a[:], 0, 2 * Q)
+                nc.vector.tensor_copy(y[0][:, start : start + count], acc[:])
+            start = start + count
+        acc = psum.tile([P, 2 * Q], F32, name="acc1_0", tag="bank5")
+        product(1, acc[:], x_a[:], 0)
         nc.scalar.copy(y[1][:, 0 : 2 * Q], acc[:])
-        acc = psum.tile([P, 2 * Q], F32, name="acc1_1", tag="bank5")
-        product(1, acc[:, 0:Q], x_code[2], 2 * Q, Q)
-        product(1, acc[:, Q : 2 * Q], x_code[3], 3 * Q, Q)
+        acc = psum.tile([P, 2 * Q], F32, name="acc1_1", tag="bank6")
+        product(1, acc[:, 0:Q], x_b[:], 2 * Q)
+        product(1, acc[:, Q : 2 * Q], x_c[:], 3 * Q)
         nc.scalar.copy(y[1][:, 2 * Q : 4 * Q], acc[:])
 
         def gated(b, d, v0, count):
@@ -122,7 +127,7 @@ def tile_picked_sub_lin_none_sub_p_kernel(
             nc.vector.tensor_tensor(
                 term[:],
                 y[b][:].indirect(pos_t[d][:, v0 // LANES : (v0 + count) // LANES]),
-                gate_t[d][:, v0 : v0 + count],
+                gate_t[:, d, v0 : v0 + count],
                 MULT,
             )
             return term
@@ -148,7 +153,7 @@ def tile_picked_sub_lin_none_sub_p_kernel(
                 nc.tensor.transpose(back[:, c * P : (c + 1) * P], staged[:, c * P : (c + 1) * P], ident[:])
             return back
 
-        sum0 = psum.tile([P, V], F32, name="sum0", tag="bank6")
+        sum0 = psum.tile([P, V], F32, name="sum0", tag="bank7")
         for d in range(D):
             add_turned(sum0[:], gated(0, d, 0, V)[:], d == 0, d == D - 1)
         back0 = turn_back(sum0[:], "0", "bank1")
@@ -156,7 +161,7 @@ def tile_picked_sub_lin_none_sub_p_kernel(
         nc.scalar.copy(res0[:], back0[:])
         nc.sync.dma_start(out[0:P, :], res0[:])
 
-        sum1 = [psum.tile([P, H], F32, name="sum1_%d" % h, tag=("bank7", "bank0")[h]) for h in range(2)]
+        sum1 = [psum.tile([P, H], F32, name="sum1_%d" % h, tag=("bank0", "bank4")[h]) for h in range(2)]
         for d in range(D - 2):
             term = gated(1, d, 0, V)
             for h in range(2):

from contextlib import ExitStack

import concourse.mybir as mybir
from concourse.masks import make_identity

K, T, D, S, V, N = 512, 2048, 4, 1024, 512, 256
FLOPS = 2 * K * N * S
BYTES = 128 * T * 4 + 16 * T + K * N * 4 + D * V * 4 + N * V * 4 + 128 * (S + D * V) // 16 * 2

F32 = mybir.dt.float32
BF16 = mybir.dt.bfloat16
I32 = mybir.dt.int32
U32 = mybir.dt.uint32
U16 = mybir.dt.uint16
U8 = mybir.dt.uint8
FP8X4 = mybir.dt.float8_e4m3fn_x4
MULT = mybir.AluOpType.mult
ADD = mybir.AluOpType.add

P = 128
PACK = 4
LANES = 16
Q = 256
H = V // 2


def tile_picked_sub_lin_none_sub_p_kernel(
    tc, x_words, x_scales, w, gate, offs, pos1, pos2, pos3, pos4, out
):
    nc = tc.nc
    with ExitStack() as ctx:
        lists = ctx.enter_context(tc.tile_pool(name="lists", bufs=1))
        keep = ctx.enter_context(tc.tile_pool(name="keep", bufs=1))
        psum = ctx.enter_context(tc.psum_pool(name="psum", bufs=1))

        offs_t = lists.tile([P, S // LANES], U16, name="offs_t")
        pos_t = [lists.tile([P, V // LANES], U16, name="pos_t%d" % d) for d in range(D)]
        pos_in = (pos1, pos2, pos3, pos4)

        scale_win = keep.tile([P, T], U8, name="scale_win", align_bytes=64)
        ident = keep.tile([P, P], F32, name="ident")
        nc.vector.memset(scale_win[:].bitcast(I32), 0)
        nc.vector.memset(ident[:], 0.0)
        make_identity(nc, ident[:], nomemset=True)

        nc.sync.dma_start(offs_t[:], offs)
        nc.sync.dma_start(pos_t[0][:], pos_in[0])
        nc.sync.dma_start(pos_t[1][:], pos_in[1])
        for q in range(4):
            eng = nc.sync if q < 2 else nc.scalar
            eng.dma_start(scale_win[32 * q : 32 * q + 4, :].bitcast(I32), x_scales[0, 4 * q : 4 * q + 4, :].bitcast(I32))
        word_win = keep.tile([P, T], I32, name="word_win", tag="word_slot", align_bytes=64)
        nc.sync.dma_start(word_win[:], x_words[0].rearrange("p c r -> p (c r)").bitcast(I32))
        w_rows = w.rearrange("(p j) m -> p j m", j=PACK)
        w_raw = [keep.tile([P, PACK, P], F32, name="w_raw%d" % b) for b in range(2)]
        for b in range(2):
            nc.sync.dma_start(w_raw[b][:], w_rows[:, :, b * P : (b + 1) * P])
        nc.sync.dma_start(pos_t[2][:], pos_in[2])
        nc.sync.dma_start(pos_t[3][:], pos_in[3])
        gate_t = keep.tile([P, D, V], F32, name="gate_t")
        nc.sync.dma_start(gate_t[:], gate[:, 0:P, :].rearrange("d p v -> p d v"))

        x_scale = keep.tile([P, S], U8, name="x_scale", align_bytes=64)
        nc.vector.tensor_copy(x_scale[:], scale_win[:].indirect(offs_t[:]))

        def gather_words(start, count, tag):
            tile = keep.tile([P, count], U32, name="x_code%d" % start, tag=tag, align_bytes=64)
            nc.vector.tensor_copy(
                tile[:], word_win[:].bitcast(U32).indirect(offs_t[:, start // LANES : (start + count) // LANES])
            )
            return tile

        def quantize(b, in_tag, out_tag):
            grouped = keep.tile([P, P, PACK], BF16, name="grouped%d" % b, tag=in_tag, align_bytes=64)
            nc.scalar.copy(
                grouped[:].rearrange("p (c i) j -> p c j i", i=PACK),
                w_raw[b][:].rearrange("p j (c i) -> p c j i", i=PACK),
            )
            code = keep.tile([P, P], U32, name="w_code%d" % b, tag=out_tag, align_bytes=64)
            scale = keep.tile([P, P], U8, name="w_scale%d" % b, align_bytes=64)
            nc.vector.quantize_mx(
                out=code[:].bitcast(FP8X4), scales=scale[:], in_=grouped[:].rearrange("p m j -> p (m j)")
            )
            return code, scale

        x_a = gather_words(0, 2 * Q, "x_a")
        x_b = gather_words(2 * Q, Q, "x_b")
        w_mx = [quantize(0, "held", "w_code0")]
        x_c = gather_words(3 * Q, Q, "held")
        w_mx.append(quantize(1, "grouped1", "word_slot"))

        y = [keep.tile([P, S], F32, name="y%d" % b) for b in range(2)]

        def product(b, acc, codes, start):
            code, scale = w_mx[b]
            nc.tensor.matmul_mx(
                out=acc,
                lhsT=code[:].bitcast(FP8X4),
                lhsT_scale=scale[:],
                rhs=codes.bitcast(FP8X4),
                rhs_scale=x_scale[:, start : start + codes.shape[1]],
                start=True,
                stop=True,
            )

        pieces = [x_a[:, 0:Q], x_a[:, Q : 2 * Q], x_b[:], x_c[:, 0:P], x_c[:, P:Q]]
        start = 0
        for i, codes in enumerate(pieces):
            count = codes.shape[1]
            acc = psum.tile([P, count], F32, name="acc0_%d" % i, tag="bank%d" % i)
            product(0, acc[:], codes, start)
            if i in (0, 2, 3):
                nc.scalar.copy(y[0][:, start : start + count], acc[:])
            else:
                nc.vector.tensor_copy(y[0][:, start : start + count], acc[:])
            start = start + count
        acc = psum.tile([P, 2 * Q], F32, name="acc1_0", tag="bank5")
        product(1, acc[:], x_a[:], 0)
        nc.scalar.copy(y[1][:, 0 : 2 * Q], acc[:])
        acc = psum.tile([P, 2 * Q], F32, name="acc1_1", tag="bank6")
        product(1, acc[:, 0:Q], x_b[:], 2 * Q)
        product(1, acc[:, Q : 2 * Q], x_c[:], 3 * Q)
        nc.scalar.copy(y[1][:, 2 * Q : 4 * Q], acc[:])

        def gated(b, d, v0, count):
            term = keep.tile([P, count], F32, name="term%d_%d_%d" % (b, d, v0))
            nc.vector.tensor_tensor(
                term[:],
                y[b][:].indirect(pos_t[d][:, v0 // LANES : (v0 + count) // LANES]),
                gate_t[:, d, v0 : v0 + count],
                MULT,
            )
            return term

        def add_turned(bank, term, first, last):
            chunks = term.shape[1] // P
            for c in range(chunks):
                nc.tensor.matmul(
                    bank[:, c * P : (c + 1) * P],
                    term[:, c * P : (c + 1) * P],
                    ident[:],
                    start=first and c == 0,
                    stop=last and c == chunks - 1,
                    is_transpose=True,
                )

        def turn_back(bank, name, tag):
            width = bank.shape[1]
            staged = keep.tile([P, width], F32, name="staged" + name)
            nc.scalar.copy(staged[:], bank[:])
            back = psum.tile([P, width], F32, name="back" + name, tag=tag)
            for c in range(width // P):
                nc.tensor.transpose(back[:, c * P : (c + 1) * P], staged[:, c * P : (c + 1) * P], ident[:])
            return back

        sum0 = psum.tile([P, V], F32, name="sum0", tag="bank7")
        for d in range(D):
            add_turned(sum0[:], gated(0, d, 0, V)[:], d == 0, d == D - 1)
        back0 = turn_back(sum0[:], "0", "bank1")
        res0 = keep.tile([P, V], F32, name="res0")
        nc.scalar.copy(res0[:], back0[:])
        nc.sync.dma_start(out[0:P, :], res0[:])

        sum1 = [psum.tile([P, H], F32, name="sum1_%d" % h, tag=("bank0", "bank4")[h]) for h in range(2)]
        for d in range(D - 2):
            term = gated(1, d, 0, V)
            for h in range(2):
                add_turned(sum1[h][:], term[:, h * H : (h + 1) * H], d == 0, False)
        back1 = []
        for h in range(2):
            add_turned(sum1[h][:], gated(1, D - 2, h * H, H)[:], False, True)
            back1.append(turn_back(sum1[h][:], "1_%d" % h, "bank%d" % (2 + h)))
        last = [gated(1, D - 1, h * H, H) for h in range(2)]
        for h in range(2):
            res1 = keep.tile([P, H], F32, name="res1_%d" % h)
            nc.vector.tensor_tensor(res1[:], last[h][:], back1[h][:], ADD)
            nc.sync.dma_start(out[P : 2 * P, h * H : (h + 1) * H], res1[:])
